import numpy as np
import ml_dtypes


def mxq(x, axis, fmt="e4m3"):
    dtype, down = {"e4m3": (ml_dtypes.float8_e4m3fn, 7), "e5m2": (ml_dtypes.float8_e5m2, 14)}[fmt]
    v = np.moveaxis(np.asarray(x, np.float32).astype(ml_dtypes.bfloat16).astype(np.float64), axis, -1)
    blocks = v.reshape(v.shape[:-1] + (-1, 32))
    amax = np.abs(blocks).max(-1, keepdims=True)
    byte = np.maximum(np.where(amax > 0, np.frexp(amax)[1] - 1 + 127, 0) - down, 1)
    scale = np.exp2(byte - 127.0)
    codes = (blocks / scale).astype(np.float32).astype(dtype).astype(np.float64)
    return np.moveaxis((codes * scale).reshape(v.shape), -1, axis)


WIDE = False


def mx_kscale(k):
    if not WIDE:
        return np.ones(k)
    levels = np.array([10, -10, 5, -5, 0])
    if k % 512:
        return np.exp2(np.random.permutation(np.resize(levels, k // 32))).repeat(32)
    a = np.empty((k // 512, 16))
    for p in range(k // 512):
        a[p, :8] = np.random.permutation(np.resize(levels, 8))
        for g in range(8):
            far = levels[np.abs(levels - a[p, g]) >= 10]
            a[p, g + 8] = far[np.random.randint(len(far))]
    return np.exp2(a.ravel()).repeat(32)


def f64(x):
    return np.asarray(x).astype(np.float64)


def striped(idx):
    return np.tile(idx.reshape(-1, 16).T, (8, 1)).astype(np.uint16)


def unstriped(offs):
    return offs[:16].T.reshape(-1).astype(np.int64)


def pack_weight(w):
    k, n = w.shape
    w = f64(np.asarray(w, np.float32).astype(ml_dtypes.bfloat16)).reshape(k // 32, 32, n)
    amax = np.abs(w).max(1)
    byte = np.clip(np.where(amax > 0, np.frexp(amax)[1] - 1 + 127 - 7, 1), 1, 254)
    scaled = (w * np.exp2(127.0 - byte)[:, None, :]).reshape(k, n).astype(np.float32)
    words = np.ascontiguousarray(scaled.reshape(k // 512, 128, 4, n).transpose(0, 1, 3, 2)).astype(ml_dtypes.float8_e4m3fn).view(np.uint8)
    return words, np.ascontiguousarray(byte.astype(np.uint8).reshape(k // 512, 16, n))


def unpack_weight(words, scales):
    g, p, n, _ = words.shape
    vals = np.ascontiguousarray(words).view(ml_dtypes.float8_e4m3fn).astype(np.float64) * np.repeat(np.exp2(scales.astype(np.float64) - 127.0), 8, axis=1)[..., None]
    return vals.transpose(0, 1, 3, 2).reshape(g * 512, n)


def silu(v):
    return v / (1.0 + np.exp(-np.maximum(v, -700.0)))

def planes(y):
    n, m = y.shape
    v = y.astype(np.float32).astype(ml_dtypes.bfloat16).astype(np.float64).reshape(n // 32, 32, m)
    top = np.abs(v).max(1)
    byte = np.clip(np.where(top > 0, np.frexp(top)[1] - 1 + 127 - 7, 1), 1, 254)
    codes = (v * np.exp2(127.0 - byte)[:, None, :]).reshape(n, m).astype(np.float32).astype(ml_dtypes.float8_e4m3fn).view(np.uint8)
    words = codes.reshape(n // 512, 128, 4, m).transpose(0, 1, 3, 2)
    return np.ascontiguousarray(words), np.ascontiguousarray(byte.astype(np.uint8).reshape(n // 512, 16, m))


K, T, N = 512, 512, 512


def setup_inputs():
    n = np.random.standard_normal
    s = mx_kscale(K)[:, None]
    packed_xT = pack_weight(n((K, T)) * s)
    return {
        "x_words": packed_xT[0],
        "x_scales": packed_xT[1],
        "w1": (n((K, N)) / np.sqrt(K) / s).astype(np.float32),
        "w2": (n((K, N)) / np.sqrt(K) / s).astype(np.float32),
        "w3": (n((K, N)) / np.sqrt(K) / s).astype(np.float32),
        "pos1": striped(np.random.permutation(T)),
        "pos2": striped(np.random.permutation(T)),
        "pos3": striped(np.random.permutation(T)),
    }


def reference(x_words, x_scales, w1, w2, w3, pos1, pos2, pos3):
    xq = unpack_weight(x_words, x_scales)
    h = mxq(f64(w3), 0, "e4m3").T @ xq
    g = mxq(f64(w1), 0, "e4m3").T @ xq
    s = mxq(f64(w2), 0, "e4m3").T @ xq
    out_0 = silu(h[:, unstriped(pos1)] * g + s) + silu(h[:, unstriped(pos2)] * g + s) + silu(h[:, unstriped(pos3)] * g + s)
    return (out_0,) + planes(out_0)

@@ -1,0 +1,159 @@
+from contextlib import ExitStack
+
+import concourse.mybir as mybir
+from concourse.masks import make_identity
+
+F32 = mybir.dt.float32
+BF16 = mybir.dt.bfloat16
+I32 = mybir.dt.int32
+U32 = mybir.dt.uint32
+U16 = mybir.dt.uint16
+U8 = mybir.dt.uint8
+FP8X4 = mybir.dt.float8_e4m3fn_x4
+SILU = mybir.ActivationFunctionType.Silu
+MULT = mybir.AluOpType.mult
+
+P = 128
+PACK = 4
+K = T = N = 512
+STRIPS = N // P
+BLOCKS = T // P
+QUAD = 32
+SPARE = 16
+FLOPS = 3 * 2 * K * T * N
+
+
+def tile_picked_wfilmg_silu_lo_kernel(
+    tc, x_words, x_scales, w1, w2, w3, pos1, pos2, pos3, out_0, out_1, out_2
+):
+    nc = tc.nc
+    with ExitStack() as ctx:
+        keep = ctx.enter_context(tc.tile_pool(name="keep", bufs=1))
+        ring = ctx.enter_context(tc.tile_pool(name="ring", bufs=3))
+        mm_ps = ctx.enter_context(tc.psum_pool(name="mm_ps", bufs=3))
+        u_ps = ctx.enter_context(tc.psum_pool(name="u_ps", bufs=3))
+        y_ps = ctx.enter_context(tc.psum_pool(name="y_ps", bufs=2))
+
+        weights = {"h": w3, "g": w1, "s": w2}
+        lists = [keep.tile([P, T // 16], U16, name="list%d" % d) for d in range(3)]
+        x_codes = keep.tile([P, T], U32, align_bytes=64)
+        x_plane = keep.tile([P, T], U8, align_bytes=64)
+        ident = keep.tile([P, P], F32)
+        warm = keep.tile([P, 8], F32)
+        windows = [keep.tile([P, T + SPARE], F32, name="h%d" % j) for j in range(STRIPS)]
+        y_plane = keep.tile([P, P], U8, align_bytes=64)
+        y_codes = keep.tile([P, STRIPS, P], U32, align_bytes=64)
+
+        nc.gpsimd.memset(x_plane[:].bitcast(U32), 0)
+        nc.gpsimd.memset(warm[:], 0.0)
+        nc.scalar.activation(warm[:], warm[:], SILU)
+        make_identity(nc, ident[:])
+        for window in windows:
+            nc.gpsimd.memset(window[:, T:], 0.0)
+
+        raw = {}
+
+        def load(name, j0, j1):
+            tile = keep.tile([P, PACK, (j1 - j0) * P], F32, name="raw_%s%d" % (name, j0))
+            nc.sync.dma_start(tile[:], weights[name][:, j0 * P : j1 * P].rearrange("(p r) c -> p r c", r=PACK))
+            for j in range(j0, j1):
+                raw[name, j] = tile[:, :, (j - j0) * P : (j - j0 + 1) * P]
+
+        load("h", 0, 1)
+        for q in range(4):
+            nc.sync.dma_start(
+                x_plane[QUAD * q : QUAD * q + 4, :].bitcast(I32), x_scales[0, 4 * q : 4 * q + 4, :].bitcast(I32)
+            )
+        nc.sync.dma_start(x_codes[:].bitcast(I32), x_words[0].rearrange("p c r -> p (c r)").bitcast(I32))
+        load("g", 0, 1)
+        nc.sync.dma_start(lists[0][:], pos1)
+        load("s", 0, 1)
+        nc.sync.dma_start(lists[1][:], pos2)
+        nc.sync.dma_start(lists[2][:], pos3)
+        for name in weights:
+            load(name, 1, 2)
+        for name in weights:
+            load(name, 2, 4)
+
+        made = {}
+        words = out_1[0].rearrange("(j c) v r -> c j (v r)", j=STRIPS).bitcast(I32)
+
+        def project(name, j):
+            grouped = keep.tile([P, P, PACK], BF16, align_bytes=64, name="grp_%s%d" % (name, j))
+            dst = grouped[:].rearrange("p (c i) r -> p c r i", i=4)
+            src = raw[name, j].rearrange("p r (c i) -> p c r i", i=4)
+            if j > 0 and name != "h":
+                nc.scalar.copy(dst, src)
+            else:
+                nc.vector.tensor_copy(dst, src)
+            codes = keep.tile([P, P], U32, align_bytes=64, name="codes_%s%d" % (name, j))
+            plane = keep.tile([P, P], U8, align_bytes=64, name="plane_%s%d" % (name, j))
+            nc.vector.quantize_mx(
+                out=codes[:].bitcast(FP8X4), scales=plane[:], in_=grouped[:].rearrange("p c r -> p (c r)")
+            )
+            acc = mm_ps.tile([P, T], F32, name="acc")
+            nc.tensor.matmul_mx(
+                out=acc[:], lhsT=codes[:].bitcast(FP8X4), lhsT_scale=plane[:],
+                rhs=x_codes[:].bitcast(FP8X4), rhs_scale=x_plane[:], start=True, stop=True,
+            )
+            if name == "h":
+                target = windows[j][:, :T]
+            else:
+                tile = keep.tile([P, T], F32, name="%s%d" % (name, j))
+                target = tile[:]
+            nc.scalar.copy(target, acc[:])
+            made[name, j] = target
+
+        def add_transposed(bank_part, block, start, stop):
+            nc.tensor.matmul(bank_part, block, ident[:], start=start, stop=stop, is_transpose=True)
+
+        def message(j, d, y_bank):
+            u_bank = u_ps.tile([P, BLOCKS, P], F32, name="u_bank")
+            for b in range(BLOCKS):
+                add_transposed(u_bank[:, b, :], made["s", j][:, b * P : (b + 1) * P], b == 0, False)
+            scaled = ring.tile([P, T], F32, name="scaled")
+            nc.vector.tensor_tensor(scaled[:], windows[j][:].indirect(lists[d][:]), made["g", j], MULT)
+            for b in range(BLOCKS):
+                add_transposed(u_bank[:, b, :], scaled[:, b * P : (b + 1) * P], False, b == BLOCKS - 1)
+            z = ring.tile([P, PACK, P], F32, name="z")
+            nc.scalar.activation(z[:], u_bank[:].rearrange("v b (c t) -> v t (b c)", t=PACK), SILU)
+            for t in range(PACK):
+                add_transposed(y_bank[:, t, :], z[:, t, :], d == 0 and t == 0, d == 2 and t == PACK - 1)
+
+        def hand_out(j, y_bank):
+            y = ring.tile([P, PACK, P], F32, name="y")
+            nc.scalar.copy(y[:], y_bank[:])
+            rows = out_0[j * P : (j + 1) * P, :].rearrange("(c t) v -> c t v", t=PACK)
+            for b in range(BLOCKS):
+                nc.sync.dma_start(rows[:, :, b * P : (b + 1) * P], y[QUAD * b : QUAD * (b + 1), :, :])
+            rounded = ring.tile([P, P, PACK], BF16, align_bytes=64, name="rounded")
+            nc.vector.tensor_copy(
+                rounded[:].rearrange("q (c i) t -> q c t i", i=4), y[:].rearrange("q t (c i) -> q c t i", i=4)
+            )
+            nc.vector.quantize_mx(
+                out=y_codes[:, j, :].bitcast(FP8X4),
+                scales=y_plane[4 * j : P, :],
+                in_=rounded[:].rearrange("q v t -> q (v t)"),
+            )
+            if j >= STRIPS - 2:
+                strips = slice(0, j + 1) if j == STRIPS - 2 else slice(j, j + 1)
+                for b in range(BLOCKS):
+                    nc.sync.dma_start(
+                        words[:, strips, b * P : (b + 1) * P],
+                        y_codes[QUAD * b : QUAD * (b + 1), strips, :].bitcast(I32),
+                    )
+
+        for name in weights:
+            project(name, 0)
+        for j in range(STRIPS):
+            y_bank = y_ps.tile([P, PACK, P], F32, name="y_bank")
+            for d, name in enumerate(weights):
+                message(j, d, y_bank)
+                if j + 1 < STRIPS:
+                    project(name, j + 1)
+            hand_out(j, y_bank)
+
+        for b in range(BLOCKS):
+            nc.sync.dma_start(
+                out_2[0, :, b * P : (b + 1) * P].bitcast(I32), y_plane[QUAD * b : QUAD * b + 16, :].bitcast(I32)
+            )

@@ -12,6 +12,7 @@ U8 = mybir.dt.uint8
 FP8X4 = mybir.dt.float8_e4m3fn_x4
 SILU = mybir.ActivationFunctionType.Silu
 MULT = mybir.AluOpType.mult
+ADD = mybir.AluOpType.add
 
 P = 128
 PACK = 4
@@ -20,6 +21,11 @@ STRIPS = N // P
 BLOCKS = T // P
 QUAD = 32
 SPARE = 16
+HALVES = [slice(0, T // 2), slice(T // 2, T)]
+KINDS = "FVFC"
+ON_VECTOR = "hg"
+AHEAD = 2
+LAG = 1
 FLOPS = 3 * 2 * K * T * N
 
 
@@ -30,8 +36,9 @@ def tile_picked_wfilmg_silu_lo_kernel(
     with ExitStack() as ctx:
         keep = ctx.enter_context(tc.tile_pool(name="keep", bufs=1))
         ring = ctx.enter_context(tc.tile_pool(name="ring", bufs=3))
-        mm_ps = ctx.enter_context(tc.psum_pool(name="mm_ps", bufs=3))
-        u_ps = ctx.enter_context(tc.psum_pool(name="u_ps", bufs=3))
+        mm_ps = ctx.enter_context(tc.psum_pool(name="mm_ps", bufs=2))
+        s_ps = ctx.enter_context(tc.psum_pool(name="s_ps", bufs=1))
+        t_ps = ctx.enter_context(tc.psum_pool(name="t_ps", bufs=3))
         y_ps = ctx.enter_context(tc.psum_pool(name="y_ps", bufs=2))
 
         weights = {"h": w3, "g": w1, "s": w2}
@@ -44,7 +51,7 @@ def tile_picked_wfilmg_silu_lo_kernel(
         y_plane = keep.tile([P, P], U8, align_bytes=64)
         y_codes = keep.tile([P, STRIPS, P], U32, align_bytes=64)
 
-        nc.gpsimd.memset(x_plane[:].bitcast(U32), 0)
+        nc.vector.memset(x_plane[:].bitcast(U32), 0)
         nc.gpsimd.memset(warm[:], 0.0)
         nc.scalar.activation(warm[:], warm[:], SILU)
         make_identity(nc, ident[:])
@@ -53,107 +60,190 @@ def tile_picked_wfilmg_silu_lo_kernel(
 
         raw = {}
 
-        def load(name, j0, j1):
-            tile = keep.tile([P, PACK, (j1 - j0) * P], F32, name="raw_%s%d" % (name, j0))
-            nc.sync.dma_start(tile[:], weights[name][:, j0 * P : j1 * P].rearrange("(p r) c -> p r c", r=PACK))
-            for j in range(j0, j1):
-                raw[name, j] = tile[:, :, (j - j0) * P : (j - j0 + 1) * P]
+        def load(name, j):
+            tile = keep.tile([P, PACK, P], F32, name="raw_%s%d" % (name, j))
+            nc.sync.dma_start(tile[:], weights[name][:, j * P : (j + 1) * P].rearrange("(p r) c -> p r c", r=PACK))
+            raw[name, j] = tile[:]
 
-        load("h", 0, 1)
         for q in range(4):
             nc.sync.dma_start(
                 x_plane[QUAD * q : QUAD * q + 4, :].bitcast(I32), x_scales[0, 4 * q : 4 * q + 4, :].bitcast(I32)
             )
-        nc.sync.dma_start(x_codes[:].bitcast(I32), x_words[0].rearrange("p c r -> p (c r)").bitcast(I32))
-        load("g", 0, 1)
+        load("h", 0)
+        load("g", 0)
+        x_flat = x_words[0].rearrange("p c r -> p (c r)").bitcast(I32)
+        for cols in HALVES:
+            nc.sync.dma_start(x_codes[:, cols].bitcast(I32), x_flat[:, cols])
         nc.sync.dma_start(lists[0][:], pos1)
-        load("s", 0, 1)
+        load("s", 0)
         nc.sync.dma_start(lists[1][:], pos2)
         nc.sync.dma_start(lists[2][:], pos3)
-        for name in weights:
-            load(name, 1, 2)
-        for name in weights:
-            load(name, 2, 4)
+        for j in range(1, STRIPS):
+            for name in weights:
+                load(name, j)
 
         made = {}
         words = out_1[0].rearrange("(j c) v r -> c j (v r)", j=STRIPS).bitcast(I32)
+        whole = [slice(0, T)]
+        quarters = [slice(a, a + P) for a in range(0, T, P)]
+        last = 3 * STRIPS - 1
 
         def project(name, j):
             grouped = keep.tile([P, P, PACK], BF16, align_bytes=64, name="grp_%s%d" % (name, j))
             dst = grouped[:].rearrange("p (c i) r -> p c r i", i=4)
             src = raw[name, j].rearrange("p r (c i) -> p c r i", i=4)
-            if j > 0 and name != "h":
-                nc.scalar.copy(dst, src)
-            else:
+            if j == 0 or name in ON_VECTOR:
                 nc.vector.tensor_copy(dst, src)
+            else:
+                nc.scalar.copy(dst, src)
             codes = keep.tile([P, P], U32, align_bytes=64, name="codes_%s%d" % (name, j))
             plane = keep.tile([P, P], U8, align_bytes=64, name="plane_%s%d" % (name, j))
             nc.vector.quantize_mx(
                 out=codes[:].bitcast(FP8X4), scales=plane[:], in_=grouped[:].rearrange("p c r -> p (c r)")
             )
-            acc = mm_ps.tile([P, T], F32, name="acc")
-            nc.tensor.matmul_mx(
-                out=acc[:], lhsT=codes[:].bitcast(FP8X4), lhsT_scale=plane[:],
-                rhs=x_codes[:].bitcast(FP8X4), rhs_scale=x_plane[:], start=True, stop=True,
-            )
+            stays = name == "s" and KINDS[j] != "F"
             if name == "h":
                 target = windows[j][:, :T]
-            else:
+            elif not stays:
                 tile = keep.tile([P, T], F32, name="%s%d" % (name, j))
                 target = tile[:]
-            nc.scalar.copy(target, acc[:])
+            early = j == 0 and name != "s"
+            for cols in HALVES if early else whole:
+                width = cols.stop - cols.start
+                if stays:
+                    acc = s_ps.tile([P, width], F32, name="s_acc")
+                elif early and name == "g":
+                    acc = t_ps.tile([P, width], F32, name="turned")
+                else:
+                    acc = mm_ps.tile([P, width], F32, name="acc")
+                nc.tensor.matmul_mx(
+                    out=acc[:], lhsT=codes[:].bitcast(FP8X4), lhsT_scale=plane[:],
+                    rhs=x_codes[:, cols].bitcast(FP8X4), rhs_scale=x_plane[:, cols], start=True, stop=True,
+                )
+                if stays:
+                    target = acc[:]
+                elif early and name == "g":
+                    nc.vector.tensor_copy(target[:, cols], acc[:])
+                else:
+                    nc.scalar.copy(target[:, cols], acc[:])
             made[name, j] = target
 
-        def add_transposed(bank_part, block, start, stop):
-            nc.tensor.matmul(bank_part, block, ident[:], start=start, stop=stop, is_transpose=True)
+        def add_transposed(bank, source, start, stop):
+            for i in range(4):
+                nc.tensor.matmul(
+                    bank[:, i * P : (i + 1) * P], source[:, i * P : (i + 1) * P], ident[:],
+                    start=start and i == 0, stop=stop and i == 3, is_transpose=True,
+                )
 
-        def message(j, d, y_bank):
-            u_bank = u_ps.tile([P, BLOCKS, P], F32, name="u_bank")
-            for b in range(BLOCKS):
-                add_transposed(u_bank[:, b, :], made["s", j][:, b * P : (b + 1) * P], b == 0, False)
-            scaled = ring.tile([P, T], F32, name="scaled")
-            nc.vector.tensor_tensor(scaled[:], windows[j][:].indirect(lists[d][:]), made["g", j], MULT)
-            for b in range(BLOCKS):
-                add_transposed(u_bank[:, b, :], scaled[:, b * P : (b + 1) * P], False, b == BLOCKS - 1)
-            z = ring.tile([P, PACK, P], F32, name="z")
-            nc.scalar.activation(z[:], u_bank[:].rearrange("v b (c t) -> v t (b c)", t=PACK), SILU)
-            for t in range(PACK):
-                add_transposed(y_bank[:, t, :], z[:, t, :], d == 0 and t == 0, d == 2 and t == PACK - 1)
+        def dealt(bank):
+            return bank[:].rearrange("v (c t) -> v t c", t=PACK)
 
-        def hand_out(j, y_bank):
-            y = ring.tile([P, PACK, P], F32, name="y")
-            nc.scalar.copy(y[:], y_bank[:])
-            rows = out_0[j * P : (j + 1) * P, :].rearrange("(c t) v -> c t v", t=PACK)
-            for b in range(BLOCKS):
-                nc.sync.dma_start(rows[:, :, b * P : (b + 1) * P], y[QUAD * b : QUAD * (b + 1), :, :])
-            rounded = ring.tile([P, P, PACK], BF16, align_bytes=64, name="rounded")
-            nc.vector.tensor_copy(
-                rounded[:].rearrange("q (c i) t -> q c t i", i=4), y[:].rearrange("q t (c i) -> q c t i", i=4)
-            )
-            nc.vector.quantize_mx(
-                out=y_codes[:, j, :].bitcast(FP8X4),
-                scales=y_plane[4 * j : P, :],
-                in_=rounded[:].rearrange("q v t -> q (v t)"),
-            )
-            if j >= STRIPS - 2:
-                strips = slice(0, j + 1) if j == STRIPS - 2 else slice(j, j + 1)
+        def message(m):
+            j, d = divmod(m, 3)
+            scaled = ring.tile([P, T], F32, name="scaled", bufs=4)
+            z = ring.tile([P, T], F32, name="z", bufs=6)
+            made["z", m] = z
+            if KINDS[j] == "F":
+                u_bank = t_ps.tile([P, T], F32, name="turned")
+                add_transposed(u_bank, made["s", j], True, False)
+            else:
+                u = ring.tile([P, T], F32, name="u", bufs=2)
+            for cols in quarters if m == last else HALVES if m == 0 else whole:
+                offsets = lists[d][:, cols.start // 16 : cols.stop // 16]
+                nc.vector.tensor_tensor(scaled[:, cols], windows[j][:].indirect(offsets), made["g", j][:, cols], MULT)
+                if KINDS[j] != "F":
+                    nc.vector.tensor_tensor(u[:, cols], scaled[:, cols], made["s", j][:, cols], ADD)
+                    nc.scalar.activation(z[:, cols], u[:, cols], SILU)
+            if KINDS[j] == "F":
+                add_transposed(u_bank, scaled, False, True)
+                nc.scalar.activation(z[:].rearrange("v (t c) -> v t c", t=PACK), dealt(u_bank), SILU)
+
+        def quantise_result(j, grouped):
+            nc.vector.quantize_mx(out=y_codes[:, j, :].bitcast(FP8X4), scales=y_plane[4 * j : P, :], in_=grouped)
+            if j % 2:
+                strips = slice(j - 1, j + 1)
                 for b in range(BLOCKS):
                     nc.sync.dma_start(
                         words[:, strips, b * P : (b + 1) * P],
                         y_codes[QUAD * b : QUAD * (b + 1), strips, :].bitcast(I32),
                     )
 
-        for name in weights:
-            project(name, 0)
-        for j in range(STRIPS):
-            y_bank = y_ps.tile([P, PACK, P], F32, name="y_bank")
-            for d, name in enumerate(weights):
-                message(j, d, y_bank)
-                if j + 1 < STRIPS:
-                    project(name, j + 1)
-            hand_out(j, y_bank)
+        def hand_out(j, y_bank):
+            y = ring.tile([P, PACK, P], F32, name="y")
+            nc.scalar.copy(y[:].rearrange("q t v -> q (t v)"), y_bank[:])
+            rows = out_0[j * P : (j + 1) * P, :].rearrange("(c t) v -> c t v", t=PACK)
+            for b in range(BLOCKS):
+                nc.sync.dma_start(rows[:, :, b * P : (b + 1) * P], y[QUAD * b : QUAD * (b + 1), :, :])
+            rounded = ring.tile([P, P, PACK], BF16, align_bytes=64, name="grouped")
+            nc.vector.tensor_copy(
+                rounded[:].rearrange("q (c i) t -> q c t i", i=4), y[:].rearrange("q t (c i) -> q c t i", i=4)
+            )
+            quantise_result(j, rounded[:].rearrange("q v t -> q (v t)"))
+
+        def collect(m):
+            j, d = divmod(m, 3)
+            z = made["z", m]
+            if KINDS[j] == "F":
+                if d == 0:
+                    made["sum", j] = y_ps.tile([P, T], F32, name="y_bank")
+                add_transposed(made["sum", j], z, d == 0, d == 2)
+                if d == 2:
+                    hand_out(j, made["sum", j])
+            elif KINDS[j] == "V":
+                if d == 0:
+                    made["sum", j] = t_ps.tile([P, T], F32, name="turned")
+                add_transposed(made["sum", j], z, d == 0, d == 2)
+                if d == 2:
+                    summed = ring.tile([P, T], F32, name="summed")
+                    nc.scalar.copy(summed[:].rearrange("v (t c) -> v t c", t=PACK), dealt(made["sum", j]))
+                    y_bank = y_ps.tile([P, T], F32, name="y_bank")
+                    add_transposed(y_bank, summed, True, True)
+                    hand_out(j, y_bank)
+            elif d == 1:
+                pair = ring.tile([P, T], F32, name="pair")
+                nc.vector.tensor_tensor(pair[:], made["z", m - 1][:], z[:], ADD)
+                made["sum", j] = pair
+            elif d == 2:
+                y = ring.tile([P, T], F32, name="y")
+                rounded = ring.tile([P, 2, P, 2], BF16, name="rounded")
+                for n, cols in enumerate(quarters if m == last else whole):
+                    nc.vector.tensor_tensor(y[:, cols], made["sum", j][:, cols], z[:, cols], ADD)
+                    width = cols.stop - cols.start
+                    if n % 2:
+                        turned = mm_ps.tile([P, width], F32, name="acc")
+                    else:
+                        turned = t_ps.tile([P, width], F32, name="turned")
+                    for a in range(0, width, P):
+                        nc.tensor.transpose(turned[:, a : a + P], y[:, cols.start + a : cols.start + a + P], ident[:])
+                    nc.scalar.copy(
+                        rounded[:, :, cols.start // PACK : cols.stop // PACK, :],
+                        turned[:].rearrange("v (c u e) -> v u c e", u=2, e=2),
+                    )
+                nc.sync.dma_start(out_0[j * P : (j + 1) * P, :], y[:])
+                pairs = rounded[:].rearrange("v u c e -> v (u c e)").bitcast(F32)
+                back = y_ps.tile([P, 2, P], F32, name="y_bank")
+                for half in range(2):
+                    nc.tensor.transpose(back[:, half, :], pairs[:, half * P : (half + 1) * P], ident[:])
+                grouped = ring.tile([P, P * PACK], BF16, align_bytes=64, name="grouped")
+                nc.scalar.copy(
+                    grouped[:].bitcast(F32).rearrange("q (v u) -> q v u", u=2), back[:].rearrange("q u v -> q v u")
+                )
+                quantise_result(j, grouped[:])
+
+        for j in range(AHEAD):
+            for name in weights:
+                project(name, j)
+        for m in range(last + 1):
+            j, d = divmod(m, 3)
+            message(m)
+            if j + AHEAD < STRIPS:
+                project("hgs"[d], j + AHEAD)
+            if m >= LAG:
+                collect(m - LAG)
+        for m in range(last + 1 - LAG, last + 1):
+            collect(m)
 
         for b in range(BLOCKS):
-            nc.sync.dma_start(
+            nc.scalar.dma_start(
                 out_2[0, :, b * P : (b + 1) * P].bitcast(I32), y_plane[QUAD * b : QUAD * b + 16, :].bitcast(I32)
             )

@@ -17,15 +17,20 @@ ADD = mybir.AluOpType.add
 P = 128
 PACK = 4
 K = T = N = 512
+LISTS = 3
 STRIPS = N // P
 BLOCKS = T // P
 QUAD = 32
+PLANE_ROWS = 4
+PER_COLUMN = 16
 SPARE = 16
-HALVES = [slice(0, T // 2), slice(T // 2, T)]
-KINDS = "FVFC"
-ON_VECTOR = "hg"
+LAST_STRIP = STRIPS - 1
+MESSAGES = LISTS * STRIPS
 AHEAD = 2
-LAG = 1
+LAG = 2
+WHOLE = [slice(0, T)]
+HALVES = [slice(0, T // 2), slice(T // 2, T)]
+QUARTERS = [slice(b * P, (b + 1) * P) for b in range(BLOCKS)]
 FLOPS = 3 * 2 * K * T * N
 
 
@@ -36,27 +41,26 @@ def tile_picked_wfilmg_silu_lo_kernel(
     with ExitStack() as ctx:
         keep = ctx.enter_context(tc.tile_pool(name="keep", bufs=1))
         ring = ctx.enter_context(tc.tile_pool(name="ring", bufs=3))
-        mm_ps = ctx.enter_context(tc.psum_pool(name="mm_ps", bufs=2))
-        s_ps = ctx.enter_context(tc.psum_pool(name="s_ps", bufs=1))
-        t_ps = ctx.enter_context(tc.psum_pool(name="t_ps", bufs=3))
-        y_ps = ctx.enter_context(tc.psum_pool(name="y_ps", bufs=2))
+        product_ps = ctx.enter_context(tc.psum_pool(name="product_ps", bufs=3))
+        shift_ps = ctx.enter_context(tc.psum_pool(name="shift_ps", bufs=1))
+        turned_ps = ctx.enter_context(tc.psum_pool(name="turned_ps", bufs=2))
+        back_ps = ctx.enter_context(tc.psum_pool(name="back_ps", bufs=2))
 
         weights = {"h": w3, "g": w1, "s": w2}
-        lists = [keep.tile([P, T // 16], U16, name="list%d" % d) for d in range(3)]
+        lists = [keep.tile([P, T // PER_COLUMN], U16, name="list%d" % d) for d in range(LISTS)]
         x_codes = keep.tile([P, T], U32, align_bytes=64)
         x_plane = keep.tile([P, T], U8, align_bytes=64)
         ident = keep.tile([P, P], F32)
-        warm = keep.tile([P, 8], F32)
+        zeros = keep.tile([P, SPARE], F32)
         windows = [keep.tile([P, T + SPARE], F32, name="h%d" % j) for j in range(STRIPS)]
-        y_plane = keep.tile([P, P], U8, align_bytes=64)
+        y_planes = keep.tile([P, P], U8, align_bytes=64)
         y_codes = keep.tile([P, STRIPS, P], U32, align_bytes=64)
 
         nc.vector.memset(x_plane[:].bitcast(U32), 0)
-        nc.gpsimd.memset(warm[:], 0.0)
-        nc.scalar.activation(warm[:], warm[:], SILU)
-        make_identity(nc, ident[:])
+        nc.gpsimd.memset(zeros[:], 0.0)
         for window in windows:
-            nc.gpsimd.memset(window[:, T:], 0.0)
+            nc.scalar.activation(window[:, T:], zeros[:], SILU)
+        make_identity(nc, ident[:])
 
         raw = {}
 
@@ -65,185 +69,195 @@ def tile_picked_wfilmg_silu_lo_kernel(
             nc.sync.dma_start(tile[:], weights[name][:, j * P : (j + 1) * P].rearrange("(p r) c -> p r c", r=PACK))
             raw[name, j] = tile[:]
 
-        for q in range(4):
+        for q in range(P // QUAD):
             nc.sync.dma_start(
-                x_plane[QUAD * q : QUAD * q + 4, :].bitcast(I32), x_scales[0, 4 * q : 4 * q + 4, :].bitcast(I32)
+                x_plane[QUAD * q : QUAD * q + PLANE_ROWS, :].bitcast(I32),
+                x_scales[0, PLANE_ROWS * q : PLANE_ROWS * (q + 1), :].bitcast(I32),
             )
-        load("h", 0)
-        load("g", 0)
+        for name in weights:
+            load(name, 0)
         x_flat = x_words[0].rearrange("p c r -> p (c r)").bitcast(I32)
         for cols in HALVES:
             nc.sync.dma_start(x_codes[:, cols].bitcast(I32), x_flat[:, cols])
-        nc.sync.dma_start(lists[0][:], pos1)
-        load("s", 0)
-        nc.sync.dma_start(lists[1][:], pos2)
-        nc.sync.dma_start(lists[2][:], pos3)
+        for tile, pos in zip(lists, (pos1, pos2, pos3)):
+            nc.sync.dma_start(tile[:], pos)
         for j in range(1, STRIPS):
             for name in weights:
                 load(name, j)
 
-        made = {}
-        words = out_1[0].rearrange("(j c) v r -> c j (v r)", j=STRIPS).bitcast(I32)
-        whole = [slice(0, T)]
-        quarters = [slice(a, a + P) for a in range(0, T, P)]
-        last = 3 * STRIPS - 1
+        operands = {}
+        products = {}
+        activated = {}
+        sums = {}
+
+        def interleave(copy, grouped, planar):
+            copy(grouped.rearrange("p (c i) r -> p c r i", i=4), planar.rearrange("p r (c i) -> p c r i", i=4))
+
+        def quantise_weight(name, j, plane, copy):
+            grouped = keep.tile([P, P, PACK], BF16, align_bytes=64, name="grouped_%s%d" % (name, j))
+            interleave(copy, grouped[:], raw[name, j])
+            codes = keep.tile([P, P], U32, align_bytes=64, name="codes_%s%d" % (name, j))
+            nc.vector.quantize_mx(
+                out=codes[:].bitcast(FP8X4), scales=plane, in_=grouped[:].rearrange("p c r -> p (c r)")
+            )
+            operands[name, j] = (codes, plane)
+
+        def multiply(name, j, bank, cols):
+            codes, plane = operands[name, j]
+            nc.tensor.matmul_mx(
+                out=bank, lhsT=codes[:].bitcast(FP8X4), lhsT_scale=plane,
+                rhs=x_codes[:, cols].bitcast(FP8X4), rhs_scale=x_plane[:, cols], start=True, stop=True,
+            )
+
+        def home_of(name, j):
+            if name == "h":
+                return windows[j][:, :T]
+            tile = keep.tile([P, T], F32, name="%s%d" % (name, j))
+            return tile[:]
 
         def project(name, j):
-            grouped = keep.tile([P, P, PACK], BF16, align_bytes=64, name="grp_%s%d" % (name, j))
-            dst = grouped[:].rearrange("p (c i) r -> p c r i", i=4)
-            src = raw[name, j].rearrange("p r (c i) -> p c r i", i=4)
-            if j == 0 or name in ON_VECTOR:
-                nc.vector.tensor_copy(dst, src)
-            else:
-                nc.scalar.copy(dst, src)
-            codes = keep.tile([P, P], U32, align_bytes=64, name="codes_%s%d" % (name, j))
-            plane = keep.tile([P, P], U8, align_bytes=64, name="plane_%s%d" % (name, j))
-            nc.vector.quantize_mx(
-                out=codes[:].bitcast(FP8X4), scales=plane[:], in_=grouped[:].rearrange("p c r -> p (c r)")
-            )
-            stays = name == "s" and KINDS[j] != "F"
-            if name == "h":
-                target = windows[j][:, :T]
-            elif not stays:
-                tile = keep.tile([P, T], F32, name="%s%d" % (name, j))
-                target = tile[:]
-            early = j == 0 and name != "s"
-            for cols in HALVES if early else whole:
-                width = cols.stop - cols.start
-                if stays:
-                    acc = s_ps.tile([P, width], F32, name="s_acc")
-                elif early and name == "g":
-                    acc = t_ps.tile([P, width], F32, name="turned")
-                else:
-                    acc = mm_ps.tile([P, width], F32, name="acc")
-                nc.tensor.matmul_mx(
-                    out=acc[:], lhsT=codes[:].bitcast(FP8X4), lhsT_scale=plane[:],
-                    rhs=x_codes[:, cols].bitcast(FP8X4), rhs_scale=x_plane[:, cols], start=True, stop=True,
-                )
-                if stays:
-                    target = acc[:]
-                elif early and name == "g":
-                    nc.vector.tensor_copy(target[:, cols], acc[:])
-                else:
-                    nc.scalar.copy(target[:, cols], acc[:])
-            made[name, j] = target
+            if name == "s" and j == LAST_STRIP:
+                bank = shift_ps.tile([P, T], F32, name="shift")
+                multiply(name, j, bank[:], WHOLE[0])
+                products[name, j] = bank[:]
+                return
+            products[name, j] = home_of(name, j)
+            bank = product_ps.tile([P, T], F32, name="product")
+            multiply(name, j, bank[:], WHOLE[0])
+            nc.scalar.copy(products[name, j], bank[:])
+
+        def first_strip():
+            for name, pool, tag, copy in (
+                ("h", product_ps, "product", nc.scalar.copy),
+                ("g", turned_ps, "turned", nc.vector.tensor_copy),
+            ):
+                plane = keep.tile([P, P], U8, align_bytes=64, name="plane_%s0" % name)
+                quantise_weight(name, 0, plane[:], nc.vector.tensor_copy)
+                products[name, 0] = home_of(name, 0)
+                for cols in HALVES:
+                    bank = pool.tile([P, T // 2], F32, name=tag)
+                    multiply(name, 0, bank[:], cols)
+                    copy(products[name, 0][:, cols], bank[:])
+            plane = keep.tile([P, P], U8, align_bytes=64, name="plane_s0")
+            quantise_weight("s", 0, plane[:], nc.scalar.copy)
+            project("s", 0)
+
+        shared_planes = {j: keep.tile([P, P], U8, align_bytes=64, name="planes%d" % j) for j in range(1, STRIPS)}
+
+        def prepare(n, j):
+            quantise_weight(list(weights)[n], j, shared_planes[j][PLANE_ROWS * n : P, :], nc.vector.tensor_copy)
+            if n == len(weights) - 1:
+                for name in weights:
+                    project(name, j)
 
         def add_transposed(bank, source, start, stop):
-            for i in range(4):
+            for i, cols in enumerate(QUARTERS):
                 nc.tensor.matmul(
-                    bank[:, i * P : (i + 1) * P], source[:, i * P : (i + 1) * P], ident[:],
-                    start=start and i == 0, stop=stop and i == 3, is_transpose=True,
+                    bank[:, cols], source[:, cols], ident[:],
+                    start=start and i == 0, stop=stop and i == BLOCKS - 1, is_transpose=True,
                 )
-
-        def dealt(bank):
-            return bank[:].rearrange("v (c t) -> v t c", t=PACK)
 
         def message(m):
-            j, d = divmod(m, 3)
+            j, d = divmod(m, LISTS)
             scaled = ring.tile([P, T], F32, name="scaled", bufs=4)
-            z = ring.tile([P, T], F32, name="z", bufs=6)
-            made["z", m] = z
-            if KINDS[j] == "F":
-                u_bank = t_ps.tile([P, T], F32, name="turned")
-                add_transposed(u_bank, made["s", j], True, False)
+            z = ring.tile([P, T], F32, name="z", bufs=4)
+            activated[m] = z
+            if j < LAST_STRIP:
+                turned = turned_ps.tile([P, T], F32, name="turned")
+                add_transposed(turned, products["s", j], True, False)
             else:
-                u = ring.tile([P, T], F32, name="u", bufs=2)
-            for cols in quarters if m == last else HALVES if m == 0 else whole:
-                offsets = lists[d][:, cols.start // 16 : cols.stop // 16]
-                nc.vector.tensor_tensor(scaled[:, cols], windows[j][:].indirect(offsets), made["g", j][:, cols], MULT)
-                if KINDS[j] != "F":
-                    nc.vector.tensor_tensor(u[:, cols], scaled[:, cols], made["s", j][:, cols], ADD)
-                    nc.scalar.activation(z[:, cols], u[:, cols], SILU)
-            if KINDS[j] == "F":
-                add_transposed(u_bank, scaled, False, True)
-                nc.scalar.activation(z[:].rearrange("v (t c) -> v t c", t=PACK), dealt(u_bank), SILU)
+                shifted = ring.tile([P, T], F32, name="shifted", bufs=2)
+            for cols in QUARTERS if m == MESSAGES - 1 else HALVES if m == 0 else WHOLE:
+                offsets = lists[d][:, cols.start // PER_COLUMN : cols.stop // PER_COLUMN]
+                nc.vector.tensor_tensor(
+                    scaled[:, cols], windows[j][:].indirect(offsets), products["g", j][:, cols], MULT
+                )
+                if j == LAST_STRIP:
+                    nc.vector.tensor_tensor(shifted[:, cols], scaled[:, cols], products["s", j][:, cols], ADD)
+                    nc.scalar.activation(z[:, cols], shifted[:, cols], SILU)
+            if j < LAST_STRIP:
+                add_transposed(turned, scaled, False, True)
+                nc.scalar.activation(
+                    z[:].rearrange("e (t q) -> e t q", t=PACK), turned[:].rearrange("e (q t) -> e t q", t=PACK), SILU
+                )
+
+        word_rows = out_1[0].rearrange("(j c) v t -> c j (v t)", j=STRIPS).bitcast(I32)
 
         def quantise_result(j, grouped):
-            nc.vector.quantize_mx(out=y_codes[:, j, :].bitcast(FP8X4), scales=y_plane[4 * j : P, :], in_=grouped)
+            nc.vector.quantize_mx(
+                out=y_codes[:, j, :].bitcast(FP8X4), scales=y_planes[PLANE_ROWS * j : P, :], in_=grouped
+            )
             if j % 2:
                 strips = slice(j - 1, j + 1)
-                for b in range(BLOCKS):
+                for b, cols in enumerate(QUARTERS):
                     nc.sync.dma_start(
-                        words[:, strips, b * P : (b + 1) * P],
-                        y_codes[QUAD * b : QUAD * (b + 1), strips, :].bitcast(I32),
+                        word_rows[:, strips, cols], y_codes[QUAD * b : QUAD * (b + 1), strips, :].bitcast(I32)
                     )
 
-        def hand_out(j, y_bank):
+        def sum_on_tensor(j, d, z):
+            if d == 0:
+                sums[j] = back_ps.tile([P, T], F32, name="back")
+            add_transposed(sums[j], z, d == 0, d == LISTS - 1)
+            if d < LISTS - 1:
+                return
             y = ring.tile([P, PACK, P], F32, name="y")
-            nc.scalar.copy(y[:].rearrange("q t v -> q (t v)"), y_bank[:])
+            nc.scalar.copy(y[:].rearrange("q t e -> q (t e)"), sums[j][:])
             rows = out_0[j * P : (j + 1) * P, :].rearrange("(c t) v -> c t v", t=PACK)
-            for b in range(BLOCKS):
-                nc.sync.dma_start(rows[:, :, b * P : (b + 1) * P], y[QUAD * b : QUAD * (b + 1), :, :])
-            rounded = ring.tile([P, P, PACK], BF16, align_bytes=64, name="grouped")
-            nc.vector.tensor_copy(
-                rounded[:].rearrange("q (c i) t -> q c t i", i=4), y[:].rearrange("q t (c i) -> q c t i", i=4)
+            for b, cols in enumerate(QUARTERS):
+                nc.sync.dma_start(rows[:, :, cols], y[QUAD * b : QUAD * (b + 1), :, :])
+            grouped = ring.tile([P, P, PACK], BF16, align_bytes=64, name="grouped")
+            interleave(nc.scalar.copy, grouped[:], y[:])
+            quantise_result(j, grouped[:].rearrange("q e t -> q (e t)"))
+
+        def finish_last_strip(j, pair, z):
+            y = ring.tile([P, T], F32, name="y")
+            rounded = keep.tile([P, 2, P, 2], BF16)
+            for b, cols in enumerate(QUARTERS):
+                nc.vector.tensor_tensor(y[:, cols], pair[:, cols], z[:, cols], ADD)
+                if b % 2:
+                    turned = product_ps.tile([P, P], F32, name="product")
+                else:
+                    turned = turned_ps.tile([P, P], F32, name="turned")
+                nc.tensor.transpose(turned[:], y[:, cols], ident[:])
+                nc.scalar.copy(
+                    rounded[:, :, QUAD * b : QUAD * (b + 1), :], turned[:].rearrange("e (c u i) -> e u c i", u=2, i=2)
+                )
+            nc.sync.dma_start(out_0[j * P : (j + 1) * P, :], y[:])
+            row_pairs = rounded[:].rearrange("e u q i -> e (u q i)").bitcast(F32)
+            back = back_ps.tile([P, 2, P], F32, name="back")
+            for u in range(2):
+                nc.tensor.transpose(back[:, u, :], row_pairs[:, u * P : (u + 1) * P], ident[:])
+            grouped = ring.tile([P, P * PACK], BF16, align_bytes=64, name="grouped")
+            nc.scalar.copy(
+                grouped[:].bitcast(F32).rearrange("q (e u) -> q e u", u=2), back[:].rearrange("q u e -> q e u")
             )
-            quantise_result(j, rounded[:].rearrange("q v t -> q (v t)"))
+            quantise_result(j, grouped[:])
 
         def collect(m):
-            j, d = divmod(m, 3)
-            z = made["z", m]
-            if KINDS[j] == "F":
-                if d == 0:
-                    made["sum", j] = y_ps.tile([P, T], F32, name="y_bank")
-                add_transposed(made["sum", j], z, d == 0, d == 2)
-                if d == 2:
-                    hand_out(j, made["sum", j])
-            elif KINDS[j] == "V":
-                if d == 0:
-                    made["sum", j] = t_ps.tile([P, T], F32, name="turned")
-                add_transposed(made["sum", j], z, d == 0, d == 2)
-                if d == 2:
-                    summed = ring.tile([P, T], F32, name="summed")
-                    nc.scalar.copy(summed[:].rearrange("v (t c) -> v t c", t=PACK), dealt(made["sum", j]))
-                    y_bank = y_ps.tile([P, T], F32, name="y_bank")
-                    add_transposed(y_bank, summed, True, True)
-                    hand_out(j, y_bank)
+            j, d = divmod(m, LISTS)
+            if j < LAST_STRIP:
+                sum_on_tensor(j, d, activated[m])
             elif d == 1:
-                pair = ring.tile([P, T], F32, name="pair")
-                nc.vector.tensor_tensor(pair[:], made["z", m - 1][:], z[:], ADD)
-                made["sum", j] = pair
+                sums[j] = keep.tile([P, T], F32, name="pair")
+                nc.vector.tensor_tensor(sums[j][:], activated[m - 1][:], activated[m][:], ADD)
             elif d == 2:
-                y = ring.tile([P, T], F32, name="y")
-                rounded = ring.tile([P, 2, P, 2], BF16, name="rounded")
-                for n, cols in enumerate(quarters if m == last else whole):
-                    nc.vector.tensor_tensor(y[:, cols], made["sum", j][:, cols], z[:, cols], ADD)
-                    width = cols.stop - cols.start
-                    if n % 2:
-                        turned = mm_ps.tile([P, width], F32, name="acc")
-                    else:
-                        turned = t_ps.tile([P, width], F32, name="turned")
-                    for a in range(0, width, P):
-                        nc.tensor.transpose(turned[:, a : a + P], y[:, cols.start + a : cols.start + a + P], ident[:])
-                    nc.scalar.copy(
-                        rounded[:, :, cols.start // PACK : cols.stop // PACK, :],
-                        turned[:].rearrange("v (c u e) -> v u c e", u=2, e=2),
-                    )
-                nc.sync.dma_start(out_0[j * P : (j + 1) * P, :], y[:])
-                pairs = rounded[:].rearrange("v u c e -> v (u c e)").bitcast(F32)
-                back = y_ps.tile([P, 2, P], F32, name="y_bank")
-                for half in range(2):
-                    nc.tensor.transpose(back[:, half, :], pairs[:, half * P : (half + 1) * P], ident[:])
-                grouped = ring.tile([P, P * PACK], BF16, align_bytes=64, name="grouped")
-                nc.scalar.copy(
-                    grouped[:].bitcast(F32).rearrange("q (v u) -> q v u", u=2), back[:].rearrange("q u v -> q v u")
-                )
-                quantise_result(j, grouped[:])
+                finish_last_strip(j, sums[j], activated[m])
 
-        for j in range(AHEAD):
-            for name in weights:
-                project(name, j)
-        for m in range(last + 1):
-            j, d = divmod(m, 3)
+        first_strip()
+        for j in range(1, AHEAD):
+            for n in range(len(weights)):
+                prepare(n, j)
+        for m in range(MESSAGES):
+            j, d = divmod(m, LISTS)
             message(m)
             if j + AHEAD < STRIPS:
-                project("hgs"[d], j + AHEAD)
+                prepare(d, j + AHEAD)
             if m >= LAG:
                 collect(m - LAG)
-        for m in range(last + 1 - LAG, last + 1):
+        for m in range(MESSAGES - LAG, MESSAGES):
             collect(m)
 
-        for b in range(BLOCKS):
-            nc.scalar.dma_start(
-                out_2[0, :, b * P : (b + 1) * P].bitcast(I32), y_plane[QUAD * b : QUAD * b + 16, :].bitcast(I32)
+        for b, cols in enumerate(QUARTERS):
+            nc.sync.dma_start(
+                out_2[0, :, cols].bitcast(I32), y_planes[QUAD * b : QUAD * b + PLANE_ROWS * STRIPS, :].bitcast(I32)
             )

from contextlib import ExitStack

import concourse.mybir as mybir
from concourse.masks import make_identity

F32 = mybir.dt.float32
BF16 = mybir.dt.bfloat16
I32 = mybir.dt.int32
U32 = mybir.dt.uint32
U16 = mybir.dt.uint16
U8 = mybir.dt.uint8
FP8X4 = mybir.dt.float8_e4m3fn_x4
SILU = mybir.ActivationFunctionType.Silu
MULT = mybir.AluOpType.mult
ADD = mybir.AluOpType.add

P = 128
PACK = 4
K = T = N = 512
LISTS = 3
STRIPS = N // P
BLOCKS = T // P
QUAD = 32
PLANE_ROWS = 4
PER_COLUMN = 16
SPARE = 16
LAST_STRIP = STRIPS - 1
MESSAGES = LISTS * STRIPS
AHEAD = 2
LAG = 2
WHOLE = [slice(0, T)]
HALVES = [slice(0, T // 2), slice(T // 2, T)]
QUARTERS = [slice(b * P, (b + 1) * P) for b in range(BLOCKS)]
FLOPS = 3 * 2 * K * T * N


def tile_picked_wfilmg_silu_lo_kernel(
    tc, x_words, x_scales, w1, w2, w3, pos1, pos2, pos3, out_0, out_1, out_2
):
    nc = tc.nc
    with ExitStack() as ctx:
        keep = ctx.enter_context(tc.tile_pool(name="keep", bufs=1))
        ring = ctx.enter_context(tc.tile_pool(name="ring", bufs=3))
        product_ps = ctx.enter_context(tc.psum_pool(name="product_ps", bufs=3))
        shift_ps = ctx.enter_context(tc.psum_pool(name="shift_ps", bufs=1))
        turned_ps = ctx.enter_context(tc.psum_pool(name="turned_ps", bufs=2))
        back_ps = ctx.enter_context(tc.psum_pool(name="back_ps", bufs=2))

        weights = {"h": w3, "g": w1, "s": w2}
        lists = [keep.tile([P, T // PER_COLUMN], U16, name="list%d" % d) for d in range(LISTS)]
        x_codes = keep.tile([P, T], U32, align_bytes=64)
        x_plane = keep.tile([P, T], U8, align_bytes=64)
        ident = keep.tile([P, P], F32)
        zeros = keep.tile([P, SPARE], F32)
        windows = [keep.tile([P, T + SPARE], F32, name="h%d" % j) for j in range(STRIPS)]
        y_planes = keep.tile([P, P], U8, align_bytes=64)
        y_codes = keep.tile([P, STRIPS, P], U32, align_bytes=64)

        nc.vector.memset(x_plane[:].bitcast(U32), 0)
        nc.gpsimd.memset(zeros[:], 0.0)
        for window in windows:
            nc.scalar.activation(window[:, T:], zeros[:], SILU)
        make_identity(nc, ident[:])

        raw = {}

        def load(name, j):
            tile = keep.tile([P, PACK, P], F32, name="raw_%s%d" % (name, j))
            nc.sync.dma_start(tile[:], weights[name][:, j * P : (j + 1) * P].rearrange("(p r) c -> p r c", r=PACK))
            raw[name, j] = tile[:]

        for q in range(P // QUAD):
            nc.sync.dma_start(
                x_plane[QUAD * q : QUAD * q + PLANE_ROWS, :].bitcast(I32),
                x_scales[0, PLANE_ROWS * q : PLANE_ROWS * (q + 1), :].bitcast(I32),
            )
        for name in weights:
            load(name, 0)
        x_flat = x_words[0].rearrange("p c r -> p (c r)").bitcast(I32)
        for cols in HALVES:
            nc.sync.dma_start(x_codes[:, cols].bitcast(I32), x_flat[:, cols])
        for tile, pos in zip(lists, (pos1, pos2, pos3)):
            nc.sync.dma_start(tile[:], pos)
        for j in range(1, STRIPS):
            for name in weights:
                load(name, j)

        operands = {}
        products = {}
        activated = {}
        sums = {}

        def interleave(copy, grouped, planar):
            copy(grouped.rearrange("p (c i) r -> p c r i", i=4), planar.rearrange("p r (c i) -> p c r i", i=4))

        def quantise_weight(name, j, plane, copy):
            grouped = keep.tile([P, P, PACK], BF16, align_bytes=64, name="grouped_%s%d" % (name, j))
            interleave(copy, grouped[:], raw[name, j])
            codes = keep.tile([P, P], U32, align_bytes=64, name="codes_%s%d" % (name, j))
            nc.vector.quantize_mx(
                out=codes[:].bitcast(FP8X4), scales=plane, in_=grouped[:].rearrange("p c r -> p (c r)")
            )
            operands[name, j] = (codes, plane)

        def multiply(name, j, bank, cols):
            codes, plane = operands[name, j]
            nc.tensor.matmul_mx(
                out=bank, lhsT=codes[:].bitcast(FP8X4), lhsT_scale=plane,
                rhs=x_codes[:, cols].bitcast(FP8X4), rhs_scale=x_plane[:, cols], start=True, stop=True,
            )

        def home_of(name, j):
            if name == "h":
                return windows[j][:, :T]
            tile = keep.tile([P, T], F32, name="%s%d" % (name, j))
            return tile[:]

        def project(name, j):
            if name == "s" and j == LAST_STRIP:
                bank = shift_ps.tile([P, T], F32, name="shift")
                multiply(name, j, bank[:], WHOLE[0])
                products[name, j] = bank[:]
                return
            products[name, j] = home_of(name, j)
            bank = product_ps.tile([P, T], F32, name="product")
            multiply(name, j, bank[:], WHOLE[0])
            nc.scalar.copy(products[name, j], bank[:])

        def first_strip():
            for name, pool, tag, copy in (
                ("h", product_ps, "product", nc.scalar.copy),
                ("g", turned_ps, "turned", nc.vector.tensor_copy),
            ):
                plane = keep.tile([P, P], U8, align_bytes=64, name="plane_%s0" % name)
                quantise_weight(name, 0, plane[:], nc.vector.tensor_copy)
                products[name, 0] = home_of(name, 0)
                for cols in HALVES:
                    bank = pool.tile([P, T // 2], F32, name=tag)
                    multiply(name, 0, bank[:], cols)
                    copy(products[name, 0][:, cols], bank[:])
            plane = keep.tile([P, P], U8, align_bytes=64, name="plane_s0")
            quantise_weight("s", 0, plane[:], nc.scalar.copy)
            project("s", 0)

        shared_planes = {j: keep.tile([P, P], U8, align_bytes=64, name="planes%d" % j) for j in range(1, STRIPS)}

        def prepare(n, j):
            quantise_weight(list(weights)[n], j, shared_planes[j][PLANE_ROWS * n : P, :], nc.vector.tensor_copy)
            if n == len(weights) - 1:
                for name in weights:
                    project(name, j)

        def add_transposed(bank, source, start, stop):
            for i, cols in enumerate(QUARTERS):
                nc.tensor.matmul(
                    bank[:, cols], source[:, cols], ident[:],
                    start=start and i == 0, stop=stop and i == BLOCKS - 1, is_transpose=True,
                )

        def message(m):
            j, d = divmod(m, LISTS)
            scaled = ring.tile([P, T], F32, name="scaled", bufs=4)
            z = ring.tile([P, T], F32, name="z", bufs=4)
            activated[m] = z
            if j < LAST_STRIP:
                turned = turned_ps.tile([P, T], F32, name="turned")
                add_transposed(turned, products["s", j], True, False)
            else:
                shifted = ring.tile([P, T], F32, name="shifted", bufs=2)
            for cols in QUARTERS if m == MESSAGES - 1 else HALVES if m == 0 else WHOLE:
                offsets = lists[d][:, cols.start // PER_COLUMN : cols.stop // PER_COLUMN]
                nc.vector.tensor_tensor(
                    scaled[:, cols], windows[j][:].indirect(offsets), products["g", j][:, cols], MULT
                )
                if j == LAST_STRIP:
                    nc.vector.tensor_tensor(shifted[:, cols], scaled[:, cols], products["s", j][:, cols], ADD)
                    nc.scalar.activation(z[:, cols], shifted[:, cols], SILU)
            if j < LAST_STRIP:
                add_transposed(turned, scaled, False, True)
                nc.scalar.activation(
                    z[:].rearrange("e (t q) -> e t q", t=PACK), turned[:].rearrange("e (q t) -> e t q", t=PACK), SILU
                )

        word_rows = out_1[0].rearrange("(j c) v t -> c j (v t)", j=STRIPS).bitcast(I32)

        def quantise_result(j, grouped):
            nc.vector.quantize_mx(
                out=y_codes[:, j, :].bitcast(FP8X4), scales=y_planes[PLANE_ROWS * j : P, :], in_=grouped
            )
            if j % 2:
                strips = slice(j - 1, j + 1)
                for b, cols in enumerate(QUARTERS):
                    nc.sync.dma_start(
                        word_rows[:, strips, cols], y_codes[QUAD * b : QUAD * (b + 1), strips, :].bitcast(I32)
                    )

        def sum_on_tensor(j, d, z):
            if d == 0:
                sums[j] = back_ps.tile([P, T], F32, name="back")
            add_transposed(sums[j], z, d == 0, d == LISTS - 1)
            if d < LISTS - 1:
                return
            y = ring.tile([P, PACK, P], F32, name="y")
            nc.scalar.copy(y[:].rearrange("q t e -> q (t e)"), sums[j][:])
            rows = out_0[j * P : (j + 1) * P, :].rearrange("(c t) v -> c t v", t=PACK)
            for b, cols in enumerate(QUARTERS):
                nc.sync.dma_start(rows[:, :, cols], y[QUAD * b : QUAD * (b + 1), :, :])
            grouped = ring.tile([P, P, PACK], BF16, align_bytes=64, name="grouped")
            interleave(nc.scalar.copy, grouped[:], y[:])
            quantise_result(j, grouped[:].rearrange("q e t -> q (e t)"))

        def finish_last_strip(j, pair, z):
            y = ring.tile([P, T], F32, name="y")
            rounded = keep.tile([P, 2, P, 2], BF16)
            for b, cols in enumerate(QUARTERS):
                nc.vector.tensor_tensor(y[:, cols], pair[:, cols], z[:, cols], ADD)
                if b % 2:
                    turned = product_ps.tile([P, P], F32, name="product")
                else:
                    turned = turned_ps.tile([P, P], F32, name="turned")
                nc.tensor.transpose(turned[:], y[:, cols], ident[:])
                nc.scalar.copy(
                    rounded[:, :, QUAD * b : QUAD * (b + 1), :], turned[:].rearrange("e (c u i) -> e u c i", u=2, i=2)
                )
            nc.sync.dma_start(out_0[j * P : (j + 1) * P, :], y[:])
            row_pairs = rounded[:].rearrange("e u q i -> e (u q i)").bitcast(F32)
            back = back_ps.tile([P, 2, P], F32, name="back")
            for u in range(2):
                nc.tensor.transpose(back[:, u, :], row_pairs[:, u * P : (u + 1) * P], ident[:])
            grouped = ring.tile([P, P * PACK], BF16, align_bytes=64, name="grouped")
            nc.scalar.copy(
                grouped[:].bitcast(F32).rearrange("q (e u) -> q e u", u=2), back[:].rearrange("q u e -> q e u")
            )
            quantise_result(j, grouped[:])

        def collect(m):
            j, d = divmod(m, LISTS)
            if j < LAST_STRIP:
                sum_on_tensor(j, d, activated[m])
            elif d == 1:
                sums[j] = keep.tile([P, T], F32, name="pair")
                nc.vector.tensor_tensor(sums[j][:], activated[m - 1][:], activated[m][:], ADD)
            elif d == 2:
                finish_last_strip(j, sums[j], activated[m])

        first_strip()
        for j in range(1, AHEAD):
            for n in range(len(weights)):
                prepare(n, j)
        for m in range(MESSAGES):
            j, d = divmod(m, LISTS)
            message(m)
            if j + AHEAD < STRIPS:
                prepare(d, j + AHEAD)
            if m >= LAG:
                collect(m - LAG)
        for m in range(MESSAGES - LAG, MESSAGES):
            collect(m)

        for b, cols in enumerate(QUARTERS):
            nc.sync.dma_start(
                out_2[0, :, cols].bitcast(I32), y_planes[QUAD * b : QUAD * b + PLANE_ROWS * STRIPS, :].bitcast(I32)
            )
